import numpy as np
import ml_dtypes


def mxq(x, axis, fmt="e4m3"):
    dtype, down = {"e4m3": (ml_dtypes.float8_e4m3fn, 7), "e5m2": (ml_dtypes.float8_e5m2, 14)}[fmt]
    v = np.moveaxis(np.asarray(x, np.float32).astype(ml_dtypes.bfloat16).astype(np.float64), axis, -1)
    blocks = v.reshape(v.shape[:-1] + (-1, 32))
    amax = np.abs(blocks).max(-1, keepdims=True)
    byte = np.maximum(np.where(amax > 0, np.frexp(amax)[1] - 1 + 127, 0) - down, 1)
    scale = np.exp2(byte - 127.0)
    codes = (blocks / scale).astype(np.float32).astype(dtype).astype(np.float64)
    return np.moveaxis((codes * scale).reshape(v.shape), -1, axis)


WIDE = False


def mx_kscale(k):
    if not WIDE:
        return np.ones(k)
    levels = np.array([10, -10, 5, -5, 0])
    if k % 512:
        return np.exp2(np.random.permutation(np.resize(levels, k // 32))).repeat(32)
    a = np.empty((k // 512, 16))
    for p in range(k // 512):
        a[p, :8] = np.random.permutation(np.resize(levels, 8))
        for g in range(8):
            far = levels[np.abs(levels - a[p, g]) >= 10]
            a[p, g + 8] = far[np.random.randint(len(far))]
    return np.exp2(a.ravel()).repeat(32)


BF16 = ml_dtypes.bfloat16


def bf(x):
    return np.asarray(x, np.float32).astype(BF16)


def f64(x):
    return np.asarray(x).astype(np.float64)


E2M1 = np.array([0.0, 0.5, 1.0, 1.5, 2.0, 3.0, 4.0, 6.0, -0.0, -0.5, -1.0, -1.5, -2.0, -3.0, -4.0, -6.0])


def pack_weight(w, fmt):
    k, n = w.shape
    w = f64(bf(w)).reshape(k // 32, 32, n)
    amax = np.abs(w).max(1)
    if fmt == "e4m3":
        byte = np.frexp(amax)[1] - 1 + 127 - 7
    else:
        mant, ex = np.frexp(amax / 6.0)
        byte = np.where(mant > 0.5, ex, ex - 1) + 127
    byte = np.clip(np.where(amax > 0, byte, 1), 1, 254)
    scaled = (w * np.exp2(127.0 - byte)[:, None, :]).reshape(k, n).astype(np.float32)
    by_word = np.ascontiguousarray(scaled.reshape(k // 512, 128, 4, n).transpose(0, 1, 3, 2))
    if fmt == "e4m3":
        words = by_word.astype(ml_dtypes.float8_e4m3fn).view(np.uint8)
    else:
        c = by_word.astype(ml_dtypes.float4_e2m1fn).view(np.uint8) & 0xF
        words = c[..., 0::2] | (c[..., 1::2] << 4)
    return np.ascontiguousarray(words), np.ascontiguousarray(byte.astype(np.uint8).reshape(k // 512, 16, n))


def unpack_weight(words, scales, fmt):
    g, p, n, _ = words.shape
    if fmt == "e4m3":
        vals = np.ascontiguousarray(words).view(ml_dtypes.float8_e4m3fn).astype(np.float64)
    else:
        nib = np.empty((g, p, n, 4), np.uint8)
        nib[..., 0::2] = words & 0xF
        nib[..., 1::2] = words >> 4
        vals = E2M1[nib]
    vals = vals * np.repeat(np.exp2(scales.astype(np.float64) - 127.0), 8, axis=1)[..., None]
    return vals.transpose(0, 1, 3, 2).reshape(g * 512, n)
def pack4(w):
    words, scales = pack_weight(w, "e2m1")
    return words.reshape(words.shape[0], 128, -1), scales


def unpack4(words, scales):
    return unpack_weight(words.reshape(words.shape[0], 128, -1, 2), scales, "e2m1")


def planes(Y):
    n, m = Y.shape
    b = f64(bf(Y)).reshape(n // 32, 32, m)
    amax = np.abs(b).max(1)
    byte = np.clip(np.where(amax > 0, np.frexp(amax)[1] - 1 + 127 - 7, 1), 1, 254)
    codes = (b * np.exp2(127.0 - byte)[:, None, :]).reshape(n, m).astype(np.float32).astype(ml_dtypes.float8_e4m3fn).view(np.uint8)
    words = codes.reshape(n // 512, 128, 4, m).transpose(0, 1, 3, 2)
    return np.ascontiguousarray(words), np.ascontiguousarray(byte.astype(np.uint8).reshape(n // 512, 16, m))


B, D, H, F = 1024, 1024, 1024, 1024


def setup_inputs():
    p, t, u = mx_kscale(D), mx_kscale(H), mx_kscale(F)
    x = bf(np.random.standard_normal((B, D)) * p)
    w1_words, w1_scales = pack4(np.random.standard_normal((D, H)) / np.sqrt(D) / p[:, None] * t)
    b1 = bf(np.random.standard_normal(H) * 0.3 * t)
    w2_words, w2_scales = pack4(np.random.standard_normal((H, D)) * 1.4 / np.sqrt(H) / t[:, None])
    return {
        "x": x,
        "w1_words": w1_words,
        "w1_scales": w1_scales,
        "b1": b1,
        "w2_words": w2_words,
        "w2_scales": w2_scales,
        "xi": bf(np.random.standard_normal((B, F)) * u),
        "c": bf(np.random.standard_normal((F, D)) / np.sqrt(F) / u[:, None]),
        "fee": bf(np.random.uniform(0.2, 0.6, D)),
    }


def hedge_network(x, w1_words, w1_scales, b1, w2_words, w2_scales):
    hid = np.maximum((mxq(x, 1, "e4m3") @ unpack4(w1_words, w1_scales)) + b1[None, :], 0.0)
    return mxq(hid, 1, "e4m3") @ unpack4(w2_words, w2_scales)


def core(x, w1_words, w1_scales, b1, w2_words, w2_scales, xi, c, fee):
    z = hedge_network(f64(x), w1_words, w1_scales, f64(b1), w2_words, w2_scales)
    dw = mxq(f64(xi), 1, "e4m3") @ mxq(f64(c), 0, "e4m3")
    s = f64(fee)[None, :] * np.maximum(-z, 0.0)
    dy = z * dw - s
    return dy


def reference(x, w1_words, w1_scales, b1, w2_words, w2_scales, xi, c, fee):
    R_out = core(x, w1_words, w1_scales, b1, w2_words, w2_scales, xi, c, fee)
    words, scales = planes(R_out)
    return R_out, words, scales

from contextlib import ExitStack

import concourse.mybir as mybir
from concourse.masks import make_identity

FLOPS = 3 * 2 * 1024 * 1024 * 1024

F32 = mybir.dt.float32
BF16 = mybir.dt.bfloat16
I32 = mybir.dt.int32
U32 = mybir.dt.uint32
U8 = mybir.dt.uint8
FP8X4 = mybir.dt.float8_e4m3fn_x4
FP4X4 = mybir.dt.float4_e2m1fn_x4
ALU = mybir.AluOpType
ACT = mybir.ActivationFunctionType

P = 128
N = 512
FAST = False
Q5 = range(3,15)
CA = ("SSSS","SSSS","SSSS","SGVV")
HI = ("VV","VV","VV")
CI = ("VG","GG","GG","GG")
E0 = "SVSVSSSS"
E1 = "SSSS"
ET = "SSSS"


def tile_deepbsdeshortfeewealthincrements_x2_kernel(
    tc, x, w1_words, w1_scales, b1, w2_words, w2_scales, xi, c, fee, out_0, out_1, out_2
):
    nc = tc.nc
    with ExitStack() as ctx:
        one = ctx.enter_context(tc.tile_pool(name="one", bufs=1))
        two = ctx.enter_context(tc.tile_pool(name="two", bufs=2))
        three = ctx.enter_context(tc.tile_pool(name="three", bufs=3))
        front = ctx.enter_context(tc.psum_pool(name="front", bufs=4))
        zbank = ctx.enter_context(tc.psum_pool(name="zbank", bufs=4))
        ctx.enter_context(tc.manual_schedule())

        w1_raw = one.tile([P, 2, 2048], U8, name="w1_raw", align_bytes=64)
        w1_sraw = one.tile([P, 2, 1024], U8, name="w1_sraw", align_bytes=64)
        w1_w = one.tile([P, 2, 2048], U8, name="w1_w", align_bytes=64)
        w1_s = one.tile([P, 2, 1024], U8, name="w1_s", align_bytes=64)
        w2_w = one.tile([P, 2, 2048], U8, name="w2_w", align_bytes=64)
        w2_s = one.tile([P, 2, 1024], U8, name="w2_s", align_bytes=64)
        fee_row = one.tile([P, 1024], BF16, name="fee_row", align_bytes=64)
        ones = one.tile([P, P], BF16, name="ones", align_bytes=64)
        fee_b = one.tile([P, 1024], BF16, name="fee_b", align_bytes=64)
        b1_raw = one.tile([P, 2, 4], BF16, name="b1_raw", align_bytes=64)
        b1_col = one.tile([P, 8], F32, name="b1_col", align_bytes=64)
        ident = one.tile([P, P], F32, name="ident", align_bytes=64)
        warm = one.tile([P, 1], F32, name="warm", align_bytes=64)
        x_raw = [one.tile([P, 4, 1024], BF16, name="x_raw%d" % g, align_bytes=64) for g in range(2)]
        xi_raw = [one.tile([P, 4, 1024], BF16, name="xi_raw%d" % g, align_bytes=64) for g in range(2)]
        c_raw = [[one.tile([P, 4, N], BF16, name="c_raw%d%d" % (k, n), align_bytes=64) for n in range(2)] for k in range(2)]

        nc.vector.memset(w1_sraw[:].bitcast(I32), 0)
        nc.vector.memset(ones[:], 1.0)
        nc.vector.memset(warm[:], 0.0)
        nc.scalar.activation(out=warm[:], in_=warm[:], func=ACT.Relu)

        def load_words(dst, src, n0, n1):
            nc.sync.dma_start(
                out=dst[:, :, 2 * n0 : 2 * n1].bitcast(I32),
                in_=src.rearrange("g p b -> p g b")[:, :, 2 * n0 : 2 * n1].bitcast(I32),
            )

        def load_scales(queue, dst, src):
            for q in range(4):
                queue.dma_start(
                    out=dst[32 * q : 32 * q + 4, :, :].bitcast(I32),
                    in_=src[:, 4 * q : 4 * q + 4, :].rearrange("g q n -> q g n").bitcast(I32),
                )

        def load_rows(dst, src, g, t0, t1):
            nc.sync.dma_start(
                out=dst[:, t0:t1, :],
                in_=src[N * g : N * (g + 1), :].rearrange("(p t) k -> p t k", t=4)[:, t0:t1, :],
            )

        def load_c(k, n):
            nc.sync.dma_start(
                out=c_raw[k][n][:],
                in_=c[N * k : N * (k + 1), N * n : N * (n + 1)].rearrange("(p j) w -> p j w", j=4),
            )

        make_identity(nc, ident[:])
        nc.gpsimd.memset(fee_row[:].bitcast(I32), 0)
        nc.gpsimd.memset(w2_s[:].bitcast(I32), 0)
        load_words(w1_raw, w1_words, 0, 512)
        load_rows(x_raw[0], x, 0, 0, 1)
        load_scales(nc.sync, w1_sraw, w1_scales)
        load_rows(x_raw[0], x, 0, 1, 2)
        load_rows(x_raw[0], x, 0, 2, 4)
        load_words(w1_raw, w1_words, 512, 1024)
        nc.sync.dma_start(out=b1_raw[:], in_=b1.rearrange("(g p t) -> p g t", g=2, t=4))
        nc.sync.dma_start(out=fee_row[0:1, :], in_=fee.rearrange("(o d) -> o d", o=1))
        load_rows(xi_raw[0], xi, 0, 0, 2)
        load_rows(xi_raw[0], xi, 0, 2, 4)
        load_c(0, 0)
        load_c(1, 0)
        load_scales(nc.sync, w2_s, w2_scales)
        load_words(w2_w, w2_words, 0, 1024)
        load_rows(x_raw[1], x, 1, 0, 2)
        load_rows(x_raw[1], x, 1, 2, 4)
        load_c(0, 1)
        load_c(1, 1)
        load_rows(xi_raw[1], xi, 1, 0, 4)

        xt = [one.tile([P, 2, N, 4], BF16, name="xt%d" % g, align_bytes=64) for g in range(2)]
        xc = [one.tile([P, 2, N], U32, name="xc%d" % g, align_bytes=64) for g in range(2)]
        xs = [one.tile([P, 2, N], U8, name="xs%d" % g, align_bytes=64) for g in range(2)]
        xit = [one.tile([P, 4, 2, P, 4], BF16, name="xit%d" % g, align_bytes=64) for g in range(2)]
        xic = [one.tile([P, 4, 2, P], U32, name="xic%d" % g, align_bytes=64) for g in range(2)]
        xis = [one.tile([P, 4, 2, P], U8, name="xis%d" % g, align_bytes=64) for g in range(2)]
        ct = [[one.tile([P, N, 4], BF16, name="ct%d%d" % (k, n), align_bytes=64) for n in range(2)] for k in range(2)]
        cc = [[one.tile([P, N], U32, name="cc%d%d" % (k, n), align_bytes=64) for n in range(2)] for k in range(2)]
        cs = [[one.tile([P, N], U8, name="cs%d%d" % (k, n), align_bytes=64) for n in range(2)] for k in range(2)]
        hp = [[one.tile([P, 4, N], BF16, name="hp%d%d" % (g, h), align_bytes=64) for h in range(2)] for g in range(2)]
        hi = [[one.tile([P, N, 4], BF16, name="hi%d%d" % (g, h), align_bytes=64) for h in range(2)] for g in range(2)]
        hc = [[one.tile([P, N], U32, name="hc%d%d" % (g, h), align_bytes=64) for h in range(2)] for g in range(2)]
        hs = [[one.tile([P, N], U8, name="hs%d%d" % (g, h), align_bytes=64) for h in range(2)] for g in range(2)]
        os_ = [one.tile([P, 1024], U8, name="os%d" % g, align_bytes=64) for g in range(2)]

        def copy(eng, out, in_):
            if eng == "S":
                nc.scalar.copy(out=out, in_=in_)
            elif eng == "V":
                nc.vector.tensor_copy(out=out, in_=in_)
            elif out.dtype == F32:
                nc.gpsimd.tensor_copy(out=out, in_=in_)
            else:
                nc.gpsimd.tensor_scalar(out=out, in0=in_, scalar1=1.0, scalar2=1.0, op0=ALU.mult, op1=ALU.mult)

        def perm_words(h):
            for k in range(2):
                nc.vector.tensor_copy(
                    out=w1_w[:, k, 1024 * h : 1024 * (h + 1)].rearrange("p (t m b) -> p t m b", t=4, b=2),
                    in_=w1_raw[:, k, 1024 * h : 1024 * (h + 1)].rearrange("p (m t b) -> p t m b", t=4, b=2),
                )

        def perm_scales(h, eng):
            eng.tensor_copy(
                out=w1_s[:, :, N * h : N * (h + 1)].rearrange("p k (t m) -> p k t m", t=4),
                in_=w1_sraw[:, :, N * h : N * (h + 1)].rearrange("p k (m t) -> p k t m", t=4),
            )

        def turn(raw, t):
            ps = front.tile([P, 2, 2, P], F32, name="ps")
            words = raw[:, t, :].bitcast(F32)
            for k in range(2):
                for u in range(2):
                    nc.tensor.transpose(ps[:, k, u, :], words[:, 256 * k + u : 256 * (k + 1) : 2], ident[:])
            return ps

        def tx(g, t, eng):
            ps = turn(x_raw[g], t)
            copy(eng, xt[g][:, :, P * t : P * (t + 1), :].bitcast(F32).rearrange("p k r u -> p k r u"), ps[:].rearrange("p k u r -> p k r u"))

        def txi(g, t, eng):
            ps = turn(xi_raw[g], t)
            copy(eng, xit[g][:, t, :, :, :].bitcast(F32), ps[:].rearrange("p k u r -> p k r u"))

        def qx(g, t):
            for k in range(2):
                nc.vector.quantize_mx(
                    out=xc[g][:, k, P * t : P * (t + 1)].bitcast(FP8X4),
                    scales=xs[g][:, k, P * t : P * (t + 1)],
                    in_=xt[g][:, k, P * t : P * (t + 1), :].rearrange("p r j -> p (r j)"),
                )

        def qxi(g, t):
            nc.vector.quantize_mx(
                out=xic[g][:, t, :, :].rearrange("p k r -> p (k r)").bitcast(FP8X4),
                scales=xis[g][:, t, :, :].rearrange("p k r -> p (k r)"),
                in_=xit[g][:, t, :, :, :].rearrange("p k r j -> p (k r j)"),
            )

        def s1(g, h, t, eng):
            ps = front.tile([P, N], F32, name="ps")
            col = 4 * h + t
            for k in range(2):
                nc.tensor.matmul_mx(
                    out=ps[:],
                    lhsT=w1_w[:, k, 256 * col : 256 * (col + 1)].bitcast(FP4X4),
                    lhsT_scale=w1_s[:, k, P * col : P * (col + 1)],
                    rhs=xc[g][:, k, :].bitcast(FP8X4),
                    rhs_scale=xs[g][:, k, :],
                    start=(k == 0),
                    stop=(k == 1),
                )
            dst = hp[g][h][:, t, :]
            if eng == "S":
                nc.scalar.activation(out=dst, in_=ps[:], func=ACT.Relu, bias=b1_col[:, col : col + 1])
            else:
                nc.vector.tensor_scalar(out=dst, in0=ps[:], scalar1=b1_col[:, col : col + 1], scalar2=0.0, op0=ALU.add, op1=ALU.max)

        def inter(dst, src, part, parts, eng):
            w = N // parts
            sl = slice(w * part, w * (part + 1))
            copy(
                eng,
                dst[:, sl, :].rearrange("p (c i) j -> p c j i", i=4) if FAST else dst[:, sl, :],
                src[:, :, sl].rearrange("p j (c i) -> p c j i", i=4) if FAST else src[:, :, sl].rearrange("p j c -> p c j"),
            )

        def quant(codes, scales, src):
            nc.vector.quantize_mx(out=codes.bitcast(FP8X4), scales=scales, in_=src.rearrange("p c j -> p (c j)"))

        def hint(g, h, engs):
            for i, e in enumerate(engs):
                inter(hi[g][h], hp[g][h], i, len(engs), e)

        def hq(g, h, a=0, b=N):
            quant(hc[g][h][:, a:b], hs[g][h][:, a:b], hi[g][h][:, a:b, :])

        def cint(k, n, engs):
            for i, e in enumerate(engs):
                inter(ct[k][n], c_raw[k][n], i, len(engs), e)

        def cq(k, n):
            quant(cc[k][n][:], cs[k][n][:], ct[k][n][:])

        units = [(g, n, t) for g in range(2) for n in range(2) for t in range(4)]
        dwp, zp, mt, ut, ot = {}, {}, {}, {}, {}

        def mm(ps, lc, ls, rc, rs):
            for k in range(2):
                nc.tensor.matmul_mx(out=ps[:], lhsT=lc[k], lhsT_scale=ls[k], rhs=rc[k], rhs_scale=rs[k], start=(k == 0), stop=(k == 1))

        def dw(i):
            g, n, t = units[i]
            ps = front.tile([P, N], F32, name="ps")
            mm(
                ps,
                [xic[g][:, t, k, :].bitcast(FP8X4) for k in range(2)],
                [xis[g][:, t, k, :] for k in range(2)],
                [cc[k][n][:].bitcast(FP8X4) for k in range(2)],
                [cs[k][n][:] for k in range(2)],
            )
            dwp[i] = ps
            if i in Q5:
                d = three.tile([P, N], F32, name="dws")
                nc.scalar.copy(out=d[:], in_=ps[:])
                dwp[i] = d

        def zz(i):
            g, n, t = units[i]
            ps = zbank.tile([P, N], F32, name="zp")
            mm(
                ps,
                [hc[g][h][:, P * t : P * (t + 1)].bitcast(FP8X4) for h in range(2)],
                [hs[g][h][:, P * t : P * (t + 1)] for h in range(2)],
                [w2_w[:, h, 1024 * n : 1024 * (n + 1)].bitcast(FP4X4) for h in range(2)],
                [w2_s[:, h, N * n : N * (n + 1)] for h in range(2)],
            )
            zp[i] = ps

        def em(i):
            g, n, t = units[i]
            m = three.tile([P, N], BF16, name="m")
            nc.vector.scalar_tensor_tensor(out=m[:], in0=zp[i][:], scalar=0.0, in1=fee_b[:, N * n : N * (n + 1)], op0=ALU.is_lt, op1=ALU.mult)
            mt[i] = m

        def tail_unit(i):
            g, n, t = units[i]
            o = ot[(g, n)]
            b = two.tile([P, N, 4], BF16, name="ob", align_bytes=64)
            cd = two.tile([P, N], U32, name="oc", align_bytes=64)
            u = three.tile([P, N], F32, name="u")
            half = N // 2
            for f in range(2):
                sl = slice(half * f, half * (f + 1))
                nc.vector.tensor_tensor(out=u[:, sl], in0=dwp[i][:, sl], in1=mt[i][:, sl], op=ALU.add)
            for f in range(2):
                sl = slice(half * f, half * (f + 1))
                nc.vector.tensor_tensor(out=o[:, t, sl], in0=zp[i][:, sl], in1=u[:, sl], op=ALU.mult)
            nc.sync.dma_start(
                out=out_0[N * g : N * (g + 1), N * n : N * (n + 1)].rearrange("(p t) m -> p t m", t=4)[:, t, :],
                in_=o[:, t, :],
            )
            for j, e in enumerate(CA[3]):
                inter(b, o, j, len(CA[3]), e)
            for f in range(2):
                sl = slice(half * f, half * (f + 1))
                quant(cd[:, sl], os_[g][:, N * n + half * f : N * n + half * (f + 1)], b[:, sl, :])
            nc.sync.dma_start(
                out=out_1[g, :, N * n : N * (n + 1), :].rearrange("p m t -> p (m t)").bitcast(I32),
                in_=cd[:].bitcast(I32),
            )
            for q in range(4):
                nc.sync.dma_start(out=out_2[g, 4 * q : 4 * q + 4, :].bitcast(I32), in_=os_[g][32 * q : 32 * q + 4, :].bitcast(I32))

        def eu(i):
            u = three.tile([P, N], F32, name="u")
            (nc.gpsimd if i in Q5 else nc.vector).tensor_tensor(out=u[:], in0=dwp[i][:], in1=mt[i][:], op=ALU.add)
            ut[i] = u

        def eo(i):
            g, n, t = units[i]
            if t == 0:
                o = two.tile([P, 4, N], F32, name="o")
                ot[(g, n)] = o
            o = ot[(g, n)]
            nc.vector.tensor_tensor(out=o[:, t, :], in0=zp[i][:], in1=ut[i][:], op=ALU.mult)
            nc.sync.dma_start(
                out=out_0[N * g : N * (g + 1), N * n : N * (n + 1)].rearrange("(p t) m -> p t m", t=4)[:, t, :],
                in_=o[:, t, :],
            )

        obt, oct_ = {}, {}

        def cast(g, n, i, engs):
            if i == 0:
                b = two.tile([P, N, 4], BF16, name="ob", align_bytes=64)
                obt[(g, n)] = b
            inter(obt[(g, n)], ot[(g, n)], i, len(engs), engs[i])

        def oq(g, n, parts=1):
            cd = two.tile([P, N], U32, name="oc", align_bytes=64)
            w = N // parts
            for j in range(parts):
                quant(cd[:, w * j : w * (j + 1)], os_[g][:, N * n + w * j : N * n + w * (j + 1)], obt[(g, n)][:, w * j : w * (j + 1), :])
            nc.sync.dma_start(
                out=out_1[g, :, N * n : N * (n + 1), :].rearrange("p m t -> p (m t)").bitcast(I32),
                in_=cd[:].bitcast(I32),
            )
            if n == 1:
                for q in range(4):
                    nc.sync.dma_start(out=out_2[g, 4 * q : 4 * q + 4, :].bitcast(I32), in_=os_[g][32 * q : 32 * q + 4, :].bitcast(I32))


        perm_words(0)
        perm_scales(0, nc.vector)
        for t in range(4):
            tx(0, t, ET[t])
            qx(0, t)
        perm_words(1)
        perm_scales(1, nc.gpsimd)
        nc.vector.tensor_copy(out=b1_col[:], in_=b1_raw[:].rearrange("p g t -> p (g t)"))
        for n in range(2):
            fp = front.tile([P, N], F32, name="ps")
            nc.tensor.matmul(fp[:], lhsT=ones[:], rhs=fee_row[:, N * n : N * (n + 1)], start=True, stop=True)
            nc.scalar.copy(out=fee_b[:, N * n : N * (n + 1)], in_=fp[:])
        for t in range(4):
            s1(0, 0, t, E0[t])
        txi(0, 0, E1[0])
        txi(0, 1, E1[1])
        cint(0, 0, CI[0])
        hint(0, 0, HI[2])
        for t in range(4):
            s1(0, 1, t, E0[4 + t])
        cint(1, 0, CI[1])
        hq(0, 0)
        cq(0, 0)
        txi(0, 2, E1[2])
        txi(0, 3, E1[3])
        inter(hi[0][1], hp[0][1], 0, 2, "V")
        hq(0, 1, 0, 256)
        inter(hi[0][1], hp[0][1], 1, 2, "V")
        hq(0, 1, 256, 512)
        qxi(0, 0)
        cq(1, 0)
        tx(1, 0, "S")
        tx(1, 1, "S")
        cint(0, 1, CI[2])
        cint(1, 1, CI[3])
        zz(0)
        zz(1)
        em(0)
        qxi(0, 1)
        em(1)
        tx(1, 2, "S")
        dw(0)
        dw(1)
        eu(0)
        tx(1, 3, "S")
        qxi(0, 2)
        qxi(0, 3)
        qx(1, 0)
        qx(1, 1)
        castat = {3: [(0, 0)], 4: [(0, 1)], 5: [(0, 2)], 6: [(0, 3)], 7: [(1, 0)], 8: [(1, 1)], 9: [(1, 2)], 10: [(1, 3)], 11: [(2, 0)], 12: [(2, 1), (2, 2)], 13: [(2, 3)]}
        oqat = {7: [0], 11: [1], 14: [2]}
        pes = {
            0: [lambda: qx(1, 2), lambda: qx(1, 3), lambda: s1(1, 0, 0, "S"), lambda: s1(1, 0, 1, "S"), lambda: cq(0, 1)],
            1: [lambda: s1(1, 0, 2, "S"), lambda: s1(1, 0, 3, "S"), lambda: cq(1, 1)],
            2: [lambda: s1(1, 1, 0, "S"), lambda: s1(1, 1, 1, "S"), lambda: hint(1, 0, HI[0])],
            3: [lambda: s1(1, 1, 2, "S"), lambda: s1(1, 1, 3, "S"), lambda: hq(1, 0)],
            4: [lambda: txi(1, 0, "S"), lambda: txi(1, 1, "S"), lambda: hint(1, 1, HI[1])],
            5: [lambda: txi(1, 2, "S"), lambda: txi(1, 3, "S"), lambda: hq(1, 1), lambda: qxi(1, 0), lambda: qxi(1, 1)],
            6: [lambda: qxi(1, 2), lambda: qxi(1, 3)],
        }
        for i in range(15):
            eu(i + 1) if i + 1 < 15 else None
            if i + 2 < 16:
                zz(i + 2)
                dw(i + 2)
            eo(i)
            for f in pes.get(i, []):
                f()
            for q, j in castat.get(i, []):
                cast(q // 2, q % 2, j, CA[q])
            for q in oqat.get(i, []):
                oq(q // 2, q % 2)
            if i + 2 < 16:
                em(i + 2)
        tail_unit(15)
